import numpy as np
import ml_dtypes


def mxq(x, axis, fmt="e4m3"):
    dtype, down = {"e4m3": (ml_dtypes.float8_e4m3fn, 7), "e5m2": (ml_dtypes.float8_e5m2, 14)}[fmt]
    v = np.moveaxis(np.asarray(x, np.float32).astype(ml_dtypes.bfloat16).astype(np.float64), axis, -1)
    blocks = v.reshape(v.shape[:-1] + (-1, 32))
    amax = np.abs(blocks).max(-1, keepdims=True)
    byte = np.maximum(np.where(amax > 0, np.frexp(amax)[1] - 1 + 127, 0) - down, 1)
    scale = np.exp2(byte - 127.0)
    codes = (blocks / scale).astype(np.float32).astype(dtype).astype(np.float64)
    return np.moveaxis((codes * scale).reshape(v.shape), -1, axis)


WIDE = False


def mx_kscale(k, group=512):
    if not WIDE:
        return np.ones(k)
    levels = np.array([10, -10, 5, -5, 0])
    if group != 512:
        return np.exp2(np.random.permutation(np.resize(levels, k // group))).repeat(group)
    if k % 512:
        return np.exp2(np.random.permutation(np.resize(levels, k // 32))).repeat(32)
    a = np.empty((k // 512, 16))
    for p in range(k // 512):
        a[p, :8] = np.random.permutation(np.resize(levels, 8))
        for g in range(8):
            far = levels[np.abs(levels - a[p, g]) >= 10]
            a[p, g + 8] = far[np.random.randint(len(far))]
    return np.exp2(a.ravel()).repeat(32)


def f64(x):
    return np.asarray(x).astype(np.float64)


E2M1 = np.array([0.0, 0.5, 1.0, 1.5, 2.0, 3.0, 4.0, 6.0, -0.0, -0.5, -1.0, -1.5, -2.0, -3.0, -4.0, -6.0])


def pack_group(w):
    k, n = w.shape
    w = f64(np.asarray(w, np.float32).astype(ml_dtypes.bfloat16)).reshape(k // 32, 32, n)
    amax = np.abs(w).max(1)
    mant, ex = np.frexp(amax / 6.0)
    byte = np.clip(np.where(amax > 0, np.where(mant > 0.5, ex, ex - 1) + 127, 1), 1, 254)
    scaled = (w * np.exp2(127.0 - byte)[:, None, :]).reshape(k, n).astype(np.float32)
    c = np.ascontiguousarray(scaled.reshape(k // 4, 4, n).transpose(0, 2, 1)).astype(ml_dtypes.float4_e2m1fn).view(np.uint8) & 0xF
    return np.ascontiguousarray((c[..., 0::2] | (c[..., 1::2] << 4)).reshape(k // 4, 2 * n)), byte.astype(np.uint8)


def unpack_group(words, scales):
    p, n = words.shape[0], scales.shape[1]
    words = np.ascontiguousarray(words).reshape(p, n, 2)
    nib = np.empty((p, n, 4), np.uint8)
    nib[..., 0::2] = words & 0xF
    nib[..., 1::2] = words >> 4
    return E2M1[nib].transpose(0, 2, 1).reshape(4 * p, n) * np.repeat(np.exp2(scales.astype(np.float64) - 127.0), 32, axis=0)


G, D, M, N = 4, 256, 128, 512


def setup_inputs():
    n = np.random.standard_normal
    s = mx_kscale(D, 0)[:, None]
    w_ = [pack_group(w) for w in n((G, D, M)) / np.sqrt(D) / s]
    return {
        "x": (n((G, D, N)) * s).astype(np.float32),
        "w_words": np.stack([w[0] for w in w_]),
        "w_scales": np.stack([w[1] for w in w_]),
        "r": n((G, M, N)).astype(np.float32),
    }


def reference(x, w_words, w_scales, r):
    xq = mxq(f64(x), 1, "e4m3")
    y = np.stack([unpack_group(w_words[g], w_scales[g]) for g in range(G)]).transpose(0, 2, 1) @ xq
    y = np.square(np.maximum(y, 0.0))
    y = y + f64(r)
    return y

@@ -1,0 +1,151 @@
+from contextlib import ExitStack
+
+import concourse.mybir as mybir
+
+G, D, M, N = 4, 256, 128, 512
+FLOPS = 2 * G * D * M * N
+
+F32 = mybir.dt.float32
+BF16 = mybir.dt.bfloat16
+I32 = mybir.dt.int32
+U32 = mybir.dt.uint32
+U8 = mybir.dt.uint8
+FP8X4 = mybir.dt.float8_e4m3fn_x4
+FP4X4 = mybir.dt.float4_e2m1fn_x4
+ACT = mybir.ActivationFunctionType
+ALU = mybir.AluOpType
+
+P = 128
+PACK = 4
+ROWS = D // PACK
+PAIRS = G // 2
+HALF = N // 2
+VECTOR_COLS = {(0, 0): 336, (0, 1): 336, (1, 0): 256, (1, 1): 416}
+
+
+def tile_rows_glin_relu2_res_kernel(tc, x, w_words, w_scales, r, out):
+    nc = tc.nc
+    with ExitStack() as ctx:
+        sb = ctx.enter_context(tc.tile_pool(name="sb", bufs=1))
+        ps = ctx.enter_context(tc.psum_pool(name="ps", bufs=1))
+        ctx.enter_context(tc.manual_schedule())
+
+        raw = {(s, h): sb.tile([P, 2, N], F32, name=f"raw{s}{h}") for s in range(PAIRS) for h in range(2)}
+        packed = [sb.tile([P, N, PACK], BF16, name=f"packed{s}", align_bytes=64) for s in range(PAIRS)]
+        codes = [sb.tile([P, N], U32, name=f"codes{s}", align_bytes=64) for s in range(PAIRS)]
+        scales = [sb.tile([P, N], U8, name=f"scales{s}", align_bytes=64) for s in range(PAIRS)]
+        w_sb = sb.tile([P, PAIRS * 2 * M], U8, align_bytes=64)
+        ws_sb = sb.tile([P, PAIRS * M], U8, align_bytes=64)
+        res = [sb.tile([P, 2, N], F32, name=f"res{s}") for s in range(PAIRS)]
+        z = [ps.tile([M, N], F32, name=f"z{g}") for g in range(G)]
+        pos = [sb.tile([M, N], F32, name=f"pos{g}") for g in range(G)]
+        sq = [sb.tile([M, N], F32, name=f"sq{g}") for g in range(G)]
+        y = [sb.tile([M, N], F32, name=f"y{g}") for g in range(G)]
+
+        x_rows = x.rearrange("(s c) (p j) n -> s (c p) j n", c=2, j=PACK)
+
+        def load_x(s, h):
+            nc.sync.dma_start(out=raw[s, h][:], in_=x_rows[s, :, 2 * h : 2 * h + 2, :])
+
+        def load_r(s):
+            nc.sync.dma_start(out=res[s][:], in_=r[2 * s : 2 * s + 2].rearrange("c m n -> m c n"))
+
+        def pack(engine, s, h, cols):
+            dst = packed[s][:, cols, 2 * h : 2 * h + 2]
+            src = raw[s, h][:, :, cols].rearrange("p j n -> p n j")
+            if engine == "vector":
+                nc.vector.tensor_copy(out=dst, in_=src)
+            else:
+                nc.scalar.copy(out=dst, in_=src)
+
+        def pack_vector(s, h):
+            pack("vector", s, h, slice(0, VECTOR_COLS[s, h]))
+
+        def pack_scalar(s, h):
+            pack("scalar", s, h, slice(VECTOR_COLS[s, h], N))
+
+        def quantize(s):
+            nc.vector.quantize_mx(
+                out=codes[s][:].bitcast(FP8X4),
+                scales=scales[s][:],
+                in_=packed[s][:].rearrange("p n j -> p (n j)"),
+            )
+
+        def multiply(s):
+            for c in range(2):
+                rows = slice(ROWS * c, ROWS * (c + 1))
+                nc.tensor.matmul_mx(
+                    out=z[2 * s + c][:],
+                    lhsT=w_sb[rows, 2 * M * s : 2 * M * (s + 1)].bitcast(FP4X4),
+                    lhsT_scale=ws_sb[rows, M * s : M * (s + 1)],
+                    rhs=codes[s][rows, :].bitcast(FP8X4),
+                    rhs_scale=scales[s][rows, :],
+                    start=True,
+                    stop=True,
+                )
+
+        whole = slice(0, N)
+        halves = [slice(0, HALF), slice(HALF, N)]
+
+        def relu_scalar(g, cols):
+            nc.scalar.activation(out=pos[g][:, cols], in_=z[g][:, cols], func=ACT.Relu)
+
+        def relu_vector(g, cols):
+            nc.vector.tensor_scalar(out=pos[g][:, cols], in0=z[g][:, cols], scalar1=0.0, scalar2=None, op0=ALU.max)
+
+        def square(g, cols):
+            nc.scalar.activation(out=sq[g][:, cols], in_=pos[g][:, cols], func=ACT.Square)
+
+        def add(g, cols):
+            nc.vector.tensor_tensor(out=y[g][:, cols], in0=sq[g][:, cols], in1=res[g // 2][:, g % 2, cols], op=ALU.add)
+
+        def store(g):
+            nc.sync.dma_start(out=out[g], in_=y[g][:])
+
+        nc.vector.memset(ws_sb[:].bitcast(I32), 0)
+        load_x(0, 0)
+        load_x(0, 1)
+        scale_rows = w_scales.bitcast(I32).rearrange("(s c) f m -> s (c f) m", c=2).rearrange("s (q i) m -> q i s m", i=4)
+        for q in range(4):
+            nc.sync.dma_start(
+                out=ws_sb[32 * q : 32 * q + 4, :].bitcast(I32).rearrange("p (s m) -> p s m", s=PAIRS),
+                in_=scale_rows[q],
+            )
+        nc.sync.dma_start(
+            out=w_sb[:].bitcast(I32).rearrange("p (s b) -> p s b", s=PAIRS),
+            in_=w_words.bitcast(I32).rearrange("(s c) p b -> (c p) s b", c=2),
+        )
+        load_x(1, 0)
+        load_x(1, 1)
+        load_r(0)
+        load_r(1)
+
+        for h in range(2):
+            pack_vector(0, h)
+            pack_scalar(0, h)
+        quantize(0)
+        multiply(0)
+        pack_scalar(1, 0)
+        pack_vector(1, 0)
+        relu_scalar(0, whole)
+        pack_vector(1, 1)
+        pack_scalar(1, 1)
+        quantize(1)
+        multiply(1)
+        square(0, whole)
+        add(0, whole)
+        store(0)
+        for cols in halves:
+            relu_scalar(1, cols)
+        for cols in halves:
+            square(1, cols)
+        relu_vector(3, whole)
+        add(1, whole)
+        store(1)
+        for cols in halves:
+            relu_scalar(2, cols)
+        for g in (2, 3):
+            for cols in halves:
+                square(g, cols)
+                add(g, cols)
+            store(g)

@@ -20,7 +20,9 @@ PACK = 4
 ROWS = D // PACK
 PAIRS = G // 2
 HALF = N // 2
-VECTOR_COLS = {(0, 0): 336, (0, 1): 336, (1, 0): 256, (1, 1): 416}
+PAD = 0
+RUN = 2
+CHUNKS = [(0, 0, N), (1, 0, HALF), (1, HALF, N)]
 
 
 def tile_rows_glin_relu2_res_kernel(tc, x, w_words, w_scales, r, out):
@@ -30,122 +32,148 @@ def tile_rows_glin_relu2_res_kernel(tc, x, w_words, w_scales, r, out):
         ps = ctx.enter_context(tc.psum_pool(name="ps", bufs=1))
         ctx.enter_context(tc.manual_schedule())
 
-        raw = {(s, h): sb.tile([P, 2, N], F32, name=f"raw{s}{h}") for s in range(PAIRS) for h in range(2)}
-        packed = [sb.tile([P, N, PACK], BF16, name=f"packed{s}", align_bytes=64) for s in range(PAIRS)]
-        codes = [sb.tile([P, N], U32, name=f"codes{s}", align_bytes=64) for s in range(PAIRS)]
-        scales = [sb.tile([P, N], U8, name=f"scales{s}", align_bytes=64) for s in range(PAIRS)]
+        raw = [sb.tile([P, PACK, n1 - n0], F32, name=f"raw{u}") for u, (s, n0, n1) in enumerate(CHUNKS)]
+        packed = [
+            sb.tile([P, n1 - n0, PACK], BF16, name=f"packed{u}", align_bytes=64) for u, (s, n0, n1) in enumerate(CHUNKS)
+        ]
+        codes = sb.tile([P, PAD + PAIRS * N], U32, align_bytes=64)
+        scales = sb.tile([P, PAD + PAIRS * N], U8, align_bytes=64)
         w_sb = sb.tile([P, PAIRS * 2 * M], U8, align_bytes=64)
         ws_sb = sb.tile([P, PAIRS * M], U8, align_bytes=64)
-        res = [sb.tile([P, 2, N], F32, name=f"res{s}") for s in range(PAIRS)]
-        z = [ps.tile([M, N], F32, name=f"z{g}") for g in range(G)]
+        res = [sb.tile([M, N], F32, name=f"res{g}") for g in range(G)]
+        z = {(u, c): ps.tile([M, N], F32, name=f"z{u}{c}") for u in range(len(CHUNKS)) for c in range(2)}
         pos = [sb.tile([M, N], F32, name=f"pos{g}") for g in range(G)]
         sq = [sb.tile([M, N], F32, name=f"sq{g}") for g in range(G)]
         y = [sb.tile([M, N], F32, name=f"y{g}") for g in range(G)]
 
         x_rows = x.rearrange("(s c) (p j) n -> s (c p) j n", c=2, j=PACK)
 
-        def load_x(s, h):
-            nc.sync.dma_start(out=raw[s, h][:], in_=x_rows[s, :, 2 * h : 2 * h + 2, :])
+        def load_x(u):
+            s, n0, n1 = CHUNKS[u]
+            nc.sync.dma_start(out=raw[u][:], in_=x_rows[s, :, :, n0:n1])
 
-        def load_r(s):
-            nc.sync.dma_start(out=res[s][:], in_=r[2 * s : 2 * s + 2].rearrange("c m n -> m c n"))
+        def load_r(g):
+            nc.sync.dma_start(out=res[g][:], in_=r[g])
 
-        def pack(engine, s, h, cols):
-            dst = packed[s][:, cols, 2 * h : 2 * h + 2]
-            src = raw[s, h][:, :, cols].rearrange("p j n -> p n j")
-            if engine == "vector":
-                nc.vector.tensor_copy(out=dst, in_=src)
-            else:
-                nc.scalar.copy(out=dst, in_=src)
-
-        def pack_vector(s, h):
-            pack("vector", s, h, slice(0, VECTOR_COLS[s, h]))
-
-        def pack_scalar(s, h):
-            pack("scalar", s, h, slice(VECTOR_COLS[s, h], N))
-
-        def quantize(s):
-            nc.vector.quantize_mx(
-                out=codes[s][:].bitcast(FP8X4),
-                scales=scales[s][:],
-                in_=packed[s][:].rearrange("p n j -> p (n j)"),
+        def load_weights():
+            scale_rows = w_scales.bitcast(I32).rearrange("(s c) f m -> s (c f) m", c=2)
+            scale_rows = scale_rows.rearrange("s (q i) m -> q i s m", i=4)
+            for q in range(4):
+                nc.sync.dma_start(
+                    out=ws_sb[32 * q : 32 * q + 4, :].bitcast(I32).rearrange("p (s m) -> p s m", s=PAIRS),
+                    in_=scale_rows[q],
+                )
+            nc.sync.dma_start(
+                out=w_sb[:].bitcast(I32).rearrange("p (s b) -> p s b", s=PAIRS),
+                in_=w_words.bitcast(I32).rearrange("(s c) p b -> (c p) s b", c=2),
             )
 
-        def multiply(s):
+        def pack_views(u, a, b):
+            dst = packed[u][:, a:b, :].rearrange("p (n i) j -> p n j i", i=RUN)
+            src = raw[u][:, :, a:b].rearrange("p j (n i) -> p n j i", i=RUN)
+            return dst, src
+
+        def pack_vector(u, a, b):
+            dst, src = pack_views(u, a, b)
+            nc.vector.tensor_copy(out=dst, in_=src)
+
+        def pack_scalar(u, a, b):
+            dst, src = pack_views(u, a, b)
+            nc.scalar.copy(out=dst, in_=src)
+
+        def quantize(u, a, b):
+            s, n0, n1 = CHUNKS[u]
+            cols = slice(PAD + N * s + n0 + a, PAD + N * s + n0 + b)
+            nc.vector.quantize_mx(
+                out=codes[:, cols].bitcast(FP8X4),
+                scales=scales[:, cols],
+                in_=packed[u][:, a:b, :].rearrange("p n j -> p (n j)"),
+            )
+
+        def multiply(u):
+            s, n0, n1 = CHUNKS[u]
+            window = slice(PAD + N * s + n1 - N, PAD + N * s + n1)
             for c in range(2):
                 rows = slice(ROWS * c, ROWS * (c + 1))
                 nc.tensor.matmul_mx(
-                    out=z[2 * s + c][:],
+                    out=z[u, c][:],
                     lhsT=w_sb[rows, 2 * M * s : 2 * M * (s + 1)].bitcast(FP4X4),
                     lhsT_scale=ws_sb[rows, M * s : M * (s + 1)],
-                    rhs=codes[s][rows, :].bitcast(FP8X4),
-                    rhs_scale=scales[s][rows, :],
+                    rhs=codes[rows, window].bitcast(FP8X4),
+                    rhs_scale=scales[rows, window],
                     start=True,
                     stop=True,
                 )
 
-        whole = slice(0, N)
-        halves = [slice(0, HALF), slice(HALF, N)]
+        def sums(u, c, a, b):
+            s, n0, n1 = CHUNKS[u]
+            a, b = (n0, n1) if a is None else (a, b)
+            return pos[2 * s + c][:, a:b], z[u, c][:, N - n1 + a : N - n1 + b]
 
-        def relu_scalar(g, cols):
-            nc.scalar.activation(out=pos[g][:, cols], in_=z[g][:, cols], func=ACT.Relu)
+        def relu_scalar(u, c, a=None, b=None):
+            dst, src = sums(u, c, a, b)
+            nc.scalar.activation(out=dst, in_=src, func=ACT.Relu)
 
-        def relu_vector(g, cols):
-            nc.vector.tensor_scalar(out=pos[g][:, cols], in0=z[g][:, cols], scalar1=0.0, scalar2=None, op0=ALU.max)
+        def relu_vector(u, c, a=None, b=None):
+            dst, src = sums(u, c, a, b)
+            nc.vector.tensor_scalar(out=dst, in0=src, scalar1=0.0, scalar2=None, op0=ALU.max)
 
-        def square(g, cols):
-            nc.scalar.activation(out=sq[g][:, cols], in_=pos[g][:, cols], func=ACT.Square)
+        def square(g, a, b):
+            nc.scalar.activation(out=sq[g][:, a:b], in_=pos[g][:, a:b], func=ACT.Square)
 
-        def add(g, cols):
-            nc.vector.tensor_tensor(out=y[g][:, cols], in0=sq[g][:, cols], in1=res[g // 2][:, g % 2, cols], op=ALU.add)
+        def add(g, a, b):
+            nc.vector.tensor_tensor(out=y[g][:, a:b], in0=sq[g][:, a:b], in1=res[g][:, a:b], op=ALU.add)
 
-        def store(g):
-            nc.sync.dma_start(out=out[g], in_=y[g][:])
+        def store(g, a, b):
+            nc.sync.dma_start(out=out[g, :, a:b], in_=y[g][:, a:b])
 
         nc.vector.memset(ws_sb[:].bitcast(I32), 0)
-        load_x(0, 0)
-        load_x(0, 1)
-        scale_rows = w_scales.bitcast(I32).rearrange("(s c) f m -> s (c f) m", c=2).rearrange("s (q i) m -> q i s m", i=4)
-        for q in range(4):
-            nc.sync.dma_start(
-                out=ws_sb[32 * q : 32 * q + 4, :].bitcast(I32).rearrange("p (s m) -> p s m", s=PAIRS),
-                in_=scale_rows[q],
-            )
-        nc.sync.dma_start(
-            out=w_sb[:].bitcast(I32).rearrange("p (s b) -> p s b", s=PAIRS),
-            in_=w_words.bitcast(I32).rearrange("(s c) p b -> (c p) s b", c=2),
-        )
-        load_x(1, 0)
-        load_x(1, 1)
+        load_x(0)
+        load_x(1)
+        load_weights()
+        load_x(2)
         load_r(0)
         load_r(1)
-
-        for h in range(2):
-            pack_vector(0, h)
-            pack_scalar(0, h)
-        quantize(0)
+        load_r(2)
+        load_r(3)
+        pack_vector(0, 0, 256)
+        pack_vector(0, 256, 312)
+        pack_scalar(0, 312, 512)
+        quantize(0, 0, 256)
+        quantize(0, 256, 512)
         multiply(0)
-        pack_scalar(1, 0)
-        pack_vector(1, 0)
-        relu_scalar(0, whole)
-        pack_vector(1, 1)
-        pack_scalar(1, 1)
-        quantize(1)
+        pack_vector(1, 0, 128)
+        pack_scalar(1, 128, 256)
+        quantize(1, 0, 256)
         multiply(1)
-        square(0, whole)
-        add(0, whole)
-        store(0)
-        for cols in halves:
-            relu_scalar(1, cols)
-        for cols in halves:
-            square(1, cols)
-        relu_vector(3, whole)
-        add(1, whole)
-        store(1)
-        for cols in halves:
-            relu_scalar(2, cols)
-        for g in (2, 3):
-            for cols in halves:
-                square(g, cols)
-                add(g, cols)
-            store(g)
+        relu_scalar(0, 0, 0, 256)
+        relu_scalar(0, 0, 256, 512)
+        relu_vector(0, 1)
+        square(0, 0, 256)
+        square(0, 256, 512)
+        pack_vector(2, 0, 128)
+        pack_vector(2, 128, 256)
+        quantize(2, 0, 128)
+        quantize(2, 128, 256)
+        multiply(2)
+        add(0, 0, 512)
+        store(0, 0, 512)
+        square(1, 0, N)
+        add(1, 0, 512)
+        store(1, 0, 512)
+        relu_scalar(1, 0)
+        relu_scalar(1, 1)
+        square(2, 0, 256)
+        square(3, 0, 256)
+        add(2, 0, 256)
+        store(2, 0, 256)
+        add(3, 0, 256)
+        store(3, 0, 256)
+        relu_scalar(2, 0)
+        relu_scalar(2, 1)
+        square(2, 256, 512)
+        square(3, 256, 512)
+        add(2, 256, 512)
+        store(2, 256, 512)
+        add(3, 256, 512)
+        store(3, 256, 512)

@@ -18,11 +18,15 @@ ALU = mybir.AluOpType
 P = 128
 PACK = 4
 ROWS = D // PACK
-PAIRS = G // 2
-HALF = N // 2
-PAD = 0
+SIDE = P // ROWS
+PAIRS = G // SIDE
+QUADRANT = 32
+WIDTH = N // 2
+CHUNKS = PAIRS * N // WIDTH
+PIECE = WIDTH // 2
 RUN = 2
-CHUNKS = [(0, 0, N), (1, 0, HALF), (1, HALF, N)]
+
+VECTOR_COLUMNS = (176, 192, WIDTH, WIDTH)
 
 
 def tile_rows_glin_relu2_res_kernel(tc, x, w_words, w_scales, r, out):
@@ -32,68 +36,72 @@ def tile_rows_glin_relu2_res_kernel(tc, x, w_words, w_scales, r, out):
         ps = ctx.enter_context(tc.psum_pool(name="ps", bufs=1))
         ctx.enter_context(tc.manual_schedule())
 
-        raw = [sb.tile([P, PACK, n1 - n0], F32, name=f"raw{u}") for u, (s, n0, n1) in enumerate(CHUNKS)]
-        packed = [
-            sb.tile([P, n1 - n0, PACK], BF16, name=f"packed{u}", align_bytes=64) for u, (s, n0, n1) in enumerate(CHUNKS)
-        ]
-        codes = sb.tile([P, PAD + PAIRS * N], U32, align_bytes=64)
-        scales = sb.tile([P, PAD + PAIRS * N], U8, align_bytes=64)
+        raw = [sb.tile([P, PACK, WIDTH], F32, name=f"raw{u}") for u in range(CHUNKS)]
+        packed = [sb.tile([P, WIDTH, PACK], BF16, name=f"packed{u}", align_bytes=64) for u in range(CHUNKS)]
+        codes = sb.tile([P, (CHUNKS + 1) * WIDTH], U32, align_bytes=64)
+        scales = sb.tile([P, (CHUNKS + 1) * WIDTH], U8, align_bytes=64)
         w_sb = sb.tile([P, PAIRS * 2 * M], U8, align_bytes=64)
         ws_sb = sb.tile([P, PAIRS * M], U8, align_bytes=64)
         res = [sb.tile([M, N], F32, name=f"res{g}") for g in range(G)]
-        z = {(u, c): ps.tile([M, N], F32, name=f"z{u}{c}") for u in range(len(CHUNKS)) for c in range(2)}
+        z = {(u, c): ps.tile([M, N], F32, name=f"z{u}{c}") for u in range(CHUNKS) for c in range(SIDE)}
         pos = [sb.tile([M, N], F32, name=f"pos{g}") for g in range(G)]
         sq = [sb.tile([M, N], F32, name=f"sq{g}") for g in range(G)]
         y = [sb.tile([M, N], F32, name=f"y{g}") for g in range(G)]
 
-        x_rows = x.rearrange("(s c) (p j) n -> s (c p) j n", c=2, j=PACK)
+        x_rows = x.rearrange("(s c) (p j) n -> s (c p) j n", c=SIDE, j=PACK)
+
+        def pair_of(u):
+            return u * WIDTH // N
+
+        def group_of(u, c):
+            return SIDE * pair_of(u) + c
+
+        def columns_of(u):
+            first = u * WIDTH % N
+            return slice(first, first + WIDTH)
 
         def load_x(u):
-            s, n0, n1 = CHUNKS[u]
-            nc.sync.dma_start(out=raw[u][:], in_=x_rows[s, :, :, n0:n1])
-
-        def load_r(g):
-            nc.sync.dma_start(out=res[g][:], in_=r[g])
+            nc.sync.dma_start(out=raw[u][:], in_=x_rows[pair_of(u), :, :, columns_of(u)])
 
         def load_weights():
-            scale_rows = w_scales.bitcast(I32).rearrange("(s c) f m -> s (c f) m", c=2)
+            scale_rows = w_scales.bitcast(I32).rearrange("(s c) f m -> s (c f) m", c=SIDE)
             scale_rows = scale_rows.rearrange("s (q i) m -> q i s m", i=4)
-            for q in range(4):
+            for q in range(P // QUADRANT):
                 nc.sync.dma_start(
-                    out=ws_sb[32 * q : 32 * q + 4, :].bitcast(I32).rearrange("p (s m) -> p s m", s=PAIRS),
+                    out=ws_sb[QUADRANT * q : QUADRANT * q + 4, :].bitcast(I32).rearrange("p (s m) -> p s m", s=PAIRS),
                     in_=scale_rows[q],
                 )
             nc.sync.dma_start(
                 out=w_sb[:].bitcast(I32).rearrange("p (s b) -> p s b", s=PAIRS),
-                in_=w_words.bitcast(I32).rearrange("(s c) p b -> (c p) s b", c=2),
+                in_=w_words.bitcast(I32).rearrange("(s c) p b -> (c p) s b", c=SIDE),
             )
 
-        def pack_views(u, a, b):
-            dst = packed[u][:, a:b, :].rearrange("p (n i) j -> p n j i", i=RUN)
-            src = raw[u][:, :, a:b].rearrange("p j (n i) -> p n j i", i=RUN)
+        def pack_views(u, first, last):
+            dst = packed[u][:, first:last, :].rearrange("p (n i) j -> p n j i", i=RUN)
+            src = raw[u][:, :, first:last].rearrange("p j (n i) -> p n j i", i=RUN)
             return dst, src
 
-        def pack_vector(u, a, b):
-            dst, src = pack_views(u, a, b)
-            nc.vector.tensor_copy(out=dst, in_=src)
+        def pack(u):
+            for first, last in ((0, PIECE), (PIECE, VECTOR_COLUMNS[u])):
+                dst, src = pack_views(u, first, last)
+                nc.vector.tensor_copy(out=dst, in_=src)
+            if VECTOR_COLUMNS[u] < WIDTH:
+                dst, src = pack_views(u, VECTOR_COLUMNS[u], WIDTH)
+                nc.scalar.copy(out=dst, in_=src)
 
-        def pack_scalar(u, a, b):
-            dst, src = pack_views(u, a, b)
-            nc.scalar.copy(out=dst, in_=src)
-
-        def quantize(u, a, b):
-            s, n0, n1 = CHUNKS[u]
-            cols = slice(PAD + N * s + n0 + a, PAD + N * s + n0 + b)
-            nc.vector.quantize_mx(
-                out=codes[:, cols].bitcast(FP8X4),
-                scales=scales[:, cols],
-                in_=packed[u][:, a:b, :].rearrange("p n j -> p (n j)"),
-            )
+        def quantize(u):
+            for first in range(0, WIDTH, PIECE):
+                cols = slice((u + 1) * WIDTH + first, (u + 1) * WIDTH + first + PIECE)
+                nc.vector.quantize_mx(
+                    out=codes[:, cols].bitcast(FP8X4),
+                    scales=scales[:, cols],
+                    in_=packed[u][:, first : first + PIECE, :].rearrange("p n j -> p (n j)"),
+                )
 
         def multiply(u):
-            s, n0, n1 = CHUNKS[u]
-            window = slice(PAD + N * s + n1 - N, PAD + N * s + n1)
-            for c in range(2):
+            s = pair_of(u)
+            window = slice((u + 2) * WIDTH - N, (u + 2) * WIDTH)
+            for c in range(SIDE):
                 rows = slice(ROWS * c, ROWS * (c + 1))
                 nc.tensor.matmul_mx(
                     out=z[u, c][:],
@@ -105,75 +113,56 @@ def tile_rows_glin_relu2_res_kernel(tc, x, w_words, w_scales, r, out):
                     stop=True,
                 )
 
-        def sums(u, c, a, b):
-            s, n0, n1 = CHUNKS[u]
-            a, b = (n0, n1) if a is None else (a, b)
-            return pos[2 * s + c][:, a:b], z[u, c][:, N - n1 + a : N - n1 + b]
+        def relu_on_scalar(u, c):
+            nc.scalar.activation(out=pos[group_of(u, c)][:, columns_of(u)], in_=z[u, c][:, N - WIDTH :], func=ACT.Relu)
 
-        def relu_scalar(u, c, a=None, b=None):
-            dst, src = sums(u, c, a, b)
-            nc.scalar.activation(out=dst, in_=src, func=ACT.Relu)
+        def relu_on_vector(u, c):
+            nc.vector.tensor_scalar(
+                out=pos[group_of(u, c)][:, columns_of(u)],
+                in0=z[u, c][:, N - WIDTH :],
+                scalar1=0.0,
+                scalar2=None,
+                op0=ALU.max,
+            )
 
-        def relu_vector(u, c, a=None, b=None):
-            dst, src = sums(u, c, a, b)
-            nc.vector.tensor_scalar(out=dst, in0=src, scalar1=0.0, scalar2=None, op0=ALU.max)
+        def square(u, c):
+            g, cols = group_of(u, c), columns_of(u)
+            nc.scalar.activation(out=sq[g][:, cols], in_=pos[g][:, cols], func=ACT.Square)
 
-        def square(g, a, b):
-            nc.scalar.activation(out=sq[g][:, a:b], in_=pos[g][:, a:b], func=ACT.Square)
-
-        def add(g, a, b):
-            nc.vector.tensor_tensor(out=y[g][:, a:b], in0=sq[g][:, a:b], in1=res[g][:, a:b], op=ALU.add)
-
-        def store(g, a, b):
-            nc.sync.dma_start(out=out[g, :, a:b], in_=y[g][:, a:b])
+        def add_and_store(g, cols):
+            nc.vector.tensor_tensor(out=y[g][:, cols], in0=sq[g][:, cols], in1=res[g][:, cols], op=ALU.add)
+            nc.sync.dma_start(out=out[g, :, cols], in_=y[g][:, cols])
 
         nc.vector.memset(ws_sb[:].bitcast(I32), 0)
+        nc.vector.memset(codes[:, :WIDTH], 0)
+        nc.vector.memset(scales[:, :WIDTH].bitcast(I32), 0)
+
         load_x(0)
-        load_x(1)
         load_weights()
-        load_x(2)
-        load_r(0)
-        load_r(1)
-        load_r(2)
-        load_r(3)
-        pack_vector(0, 0, 256)
-        pack_vector(0, 256, 312)
-        pack_scalar(0, 312, 512)
-        quantize(0, 0, 256)
-        quantize(0, 256, 512)
-        multiply(0)
-        pack_vector(1, 0, 128)
-        pack_scalar(1, 128, 256)
-        quantize(1, 0, 256)
-        multiply(1)
-        relu_scalar(0, 0, 0, 256)
-        relu_scalar(0, 0, 256, 512)
-        relu_vector(0, 1)
-        square(0, 0, 256)
-        square(0, 256, 512)
-        pack_vector(2, 0, 128)
-        pack_vector(2, 128, 256)
-        quantize(2, 0, 128)
-        quantize(2, 128, 256)
-        multiply(2)
-        add(0, 0, 512)
-        store(0, 0, 512)
-        square(1, 0, N)
-        add(1, 0, 512)
-        store(1, 0, 512)
-        relu_scalar(1, 0)
-        relu_scalar(1, 1)
-        square(2, 0, 256)
-        square(3, 0, 256)
-        add(2, 0, 256)
-        store(2, 0, 256)
-        add(3, 0, 256)
-        store(3, 0, 256)
-        relu_scalar(2, 0)
-        relu_scalar(2, 1)
-        square(2, 256, 512)
-        square(3, 256, 512)
-        add(2, 256, 512)
-        store(2, 256, 512)
-        add(3, 256, 512)
-        store(3, 256, 512)
+        for u in range(1, CHUNKS):
+            load_x(u)
+        for g in range(G):
+            nc.sync.dma_start(out=res[g][:], in_=r[g])
+
+        for u in range(CHUNKS):
+            pack(u)
+            quantize(u)
+            multiply(u)
+            if u > 0:
+                for c in range(SIDE):
+                    relu_on_scalar(u - 1, c)
+                for c in range(SIDE):
+                    square(u - 1, c)
+
+        for g in range(SIDE):
+            add_and_store(g, slice(0, N))
+
+        last_chunk = CHUNKS - 1
+        relu_on_vector(last_chunk, 0)
+        relu_on_scalar(last_chunk, 1)
+        for c in range(SIDE):
+            add_and_store(group_of(last_chunk - 1, c), columns_of(last_chunk - 1))
+        for c in range(SIDE):
+            square(last_chunk, c)
+        for c in range(SIDE):
+            add_and_store(group_of(last_chunk, c), columns_of(last_chunk))

from contextlib import ExitStack

import concourse.mybir as mybir

G, D, M, N = 4, 256, 128, 512
FLOPS = 2 * G * D * M * N

F32 = mybir.dt.float32
BF16 = mybir.dt.bfloat16
I32 = mybir.dt.int32
U32 = mybir.dt.uint32
U8 = mybir.dt.uint8
FP8X4 = mybir.dt.float8_e4m3fn_x4
FP4X4 = mybir.dt.float4_e2m1fn_x4
ACT = mybir.ActivationFunctionType
ALU = mybir.AluOpType

P = 128
PACK = 4
ROWS = D // PACK
SIDE = P // ROWS
PAIRS = G // SIDE
QUADRANT = 32
WIDTH = N // 2
CHUNKS = PAIRS * N // WIDTH
PIECE = WIDTH // 2
RUN = 2

VECTOR_COLUMNS = (176, 192, WIDTH, WIDTH)


def tile_rows_glin_relu2_res_kernel(tc, x, w_words, w_scales, r, out):
    nc = tc.nc
    with ExitStack() as ctx:
        sb = ctx.enter_context(tc.tile_pool(name="sb", bufs=1))
        ps = ctx.enter_context(tc.psum_pool(name="ps", bufs=1))
        ctx.enter_context(tc.manual_schedule())

        raw = [sb.tile([P, PACK, WIDTH], F32, name=f"raw{u}") for u in range(CHUNKS)]
        packed = [sb.tile([P, WIDTH, PACK], BF16, name=f"packed{u}", align_bytes=64) for u in range(CHUNKS)]
        codes = sb.tile([P, (CHUNKS + 1) * WIDTH], U32, align_bytes=64)
        scales = sb.tile([P, (CHUNKS + 1) * WIDTH], U8, align_bytes=64)
        w_sb = sb.tile([P, PAIRS * 2 * M], U8, align_bytes=64)
        ws_sb = sb.tile([P, PAIRS * M], U8, align_bytes=64)
        res = [sb.tile([M, N], F32, name=f"res{g}") for g in range(G)]
        z = {(u, c): ps.tile([M, N], F32, name=f"z{u}{c}") for u in range(CHUNKS) for c in range(SIDE)}
        pos = [sb.tile([M, N], F32, name=f"pos{g}") for g in range(G)]
        sq = [sb.tile([M, N], F32, name=f"sq{g}") for g in range(G)]
        y = [sb.tile([M, N], F32, name=f"y{g}") for g in range(G)]

        x_rows = x.rearrange("(s c) (p j) n -> s (c p) j n", c=SIDE, j=PACK)

        def pair_of(u):
            return u * WIDTH // N

        def group_of(u, c):
            return SIDE * pair_of(u) + c

        def columns_of(u):
            first = u * WIDTH % N
            return slice(first, first + WIDTH)

        def load_x(u):
            nc.sync.dma_start(out=raw[u][:], in_=x_rows[pair_of(u), :, :, columns_of(u)])

        def load_weights():
            scale_rows = w_scales.bitcast(I32).rearrange("(s c) f m -> s (c f) m", c=SIDE)
            scale_rows = scale_rows.rearrange("s (q i) m -> q i s m", i=4)
            for q in range(P // QUADRANT):
                nc.sync.dma_start(
                    out=ws_sb[QUADRANT * q : QUADRANT * q + 4, :].bitcast(I32).rearrange("p (s m) -> p s m", s=PAIRS),
                    in_=scale_rows[q],
                )
            nc.sync.dma_start(
                out=w_sb[:].bitcast(I32).rearrange("p (s b) -> p s b", s=PAIRS),
                in_=w_words.bitcast(I32).rearrange("(s c) p b -> (c p) s b", c=SIDE),
            )

        def pack_views(u, first, last):
            dst = packed[u][:, first:last, :].rearrange("p (n i) j -> p n j i", i=RUN)
            src = raw[u][:, :, first:last].rearrange("p j (n i) -> p n j i", i=RUN)
            return dst, src

        def pack(u):
            for first, last in ((0, PIECE), (PIECE, VECTOR_COLUMNS[u])):
                dst, src = pack_views(u, first, last)
                nc.vector.tensor_copy(out=dst, in_=src)
            if VECTOR_COLUMNS[u] < WIDTH:
                dst, src = pack_views(u, VECTOR_COLUMNS[u], WIDTH)
                nc.scalar.copy(out=dst, in_=src)

        def quantize(u):
            for first in range(0, WIDTH, PIECE):
                cols = slice((u + 1) * WIDTH + first, (u + 1) * WIDTH + first + PIECE)
                nc.vector.quantize_mx(
                    out=codes[:, cols].bitcast(FP8X4),
                    scales=scales[:, cols],
                    in_=packed[u][:, first : first + PIECE, :].rearrange("p n j -> p (n j)"),
                )

        def multiply(u):
            s = pair_of(u)
            window = slice((u + 2) * WIDTH - N, (u + 2) * WIDTH)
            for c in range(SIDE):
                rows = slice(ROWS * c, ROWS * (c + 1))
                nc.tensor.matmul_mx(
                    out=z[u, c][:],
                    lhsT=w_sb[rows, 2 * M * s : 2 * M * (s + 1)].bitcast(FP4X4),
                    lhsT_scale=ws_sb[rows, M * s : M * (s + 1)],
                    rhs=codes[rows, window].bitcast(FP8X4),
                    rhs_scale=scales[rows, window],
                    start=True,
                    stop=True,
                )

        def relu_on_scalar(u, c):
            nc.scalar.activation(out=pos[group_of(u, c)][:, columns_of(u)], in_=z[u, c][:, N - WIDTH :], func=ACT.Relu)

        def relu_on_vector(u, c):
            nc.vector.tensor_scalar(
                out=pos[group_of(u, c)][:, columns_of(u)],
                in0=z[u, c][:, N - WIDTH :],
                scalar1=0.0,
                scalar2=None,
                op0=ALU.max,
            )

        def square(u, c):
            g, cols = group_of(u, c), columns_of(u)
            nc.scalar.activation(out=sq[g][:, cols], in_=pos[g][:, cols], func=ACT.Square)

        def add_and_store(g, cols):
            nc.vector.tensor_tensor(out=y[g][:, cols], in0=sq[g][:, cols], in1=res[g][:, cols], op=ALU.add)
            nc.sync.dma_start(out=out[g, :, cols], in_=y[g][:, cols])

        nc.vector.memset(ws_sb[:].bitcast(I32), 0)
        nc.vector.memset(codes[:, :WIDTH], 0)
        nc.vector.memset(scales[:, :WIDTH].bitcast(I32), 0)

        load_x(0)
        load_weights()
        for u in range(1, CHUNKS):
            load_x(u)
        for g in range(G):
            nc.sync.dma_start(out=res[g][:], in_=r[g])

        for u in range(CHUNKS):
            pack(u)
            quantize(u)
            multiply(u)
            if u > 0:
                for c in range(SIDE):
                    relu_on_scalar(u - 1, c)
                for c in range(SIDE):
                    square(u - 1, c)

        for g in range(SIDE):
            add_and_store(g, slice(0, N))

        last_chunk = CHUNKS - 1
        relu_on_vector(last_chunk, 0)
        relu_on_scalar(last_chunk, 1)
        for c in range(SIDE):
            add_and_store(group_of(last_chunk - 1, c), columns_of(last_chunk - 1))
        for c in range(SIDE):
            square(last_chunk, c)
        for c in range(SIDE):
            add_and_store(group_of(last_chunk, c), columns_of(last_chunk))
